import numpy as np
import ml_dtypes


def mxq(x, axis, fmt="e4m3"):
    dtype, down = {"e4m3": (ml_dtypes.float8_e4m3fn, 7), "e5m2": (ml_dtypes.float8_e5m2, 14)}[fmt]
    v = np.moveaxis(np.asarray(x, np.float32).astype(ml_dtypes.bfloat16).astype(np.float64), axis, -1)
    blocks = v.reshape(v.shape[:-1] + (-1, 32))
    amax = np.abs(blocks).max(-1, keepdims=True)
    byte = np.maximum(np.where(amax > 0, np.frexp(amax)[1] - 1 + 127, 0) - down, 1)
    scale = np.exp2(byte - 127.0)
    codes = (blocks / scale).astype(np.float32).astype(dtype).astype(np.float64)
    return np.moveaxis((codes * scale).reshape(v.shape), -1, axis)


WIDE = False


def mx_kscale(k):
    if not WIDE:
        return np.ones(k)
    levels = np.array([10, -10, 5, -5, 0])
    if k % 512:
        return np.exp2(np.random.permutation(np.resize(levels, k // 32))).repeat(32)
    a = np.empty((k // 512, 16))
    for p in range(k // 512):
        a[p, :8] = np.random.permutation(np.resize(levels, 8))
        for g in range(8):
            far = levels[np.abs(levels - a[p, g]) >= 10]
            a[p, g + 8] = far[np.random.randint(len(far))]
    return np.exp2(a.ravel()).repeat(32)


BF16 = ml_dtypes.bfloat16


def bf(x):
    return np.asarray(x, np.float32).astype(BF16)


def f64(x):
    return np.asarray(x).astype(np.float64)

E4M3FN = np.array([(-1.0 if i & 128 else 1.0) * ((1.0 + (i & 7) / 8.0) * 2.0 ** (((i >> 3) & 15) - 7) if i & 120 else (i & 7) * 2.0 ** -9) for i in range(256)])


def e4m3fn_bytes(y):
    return np.clip(np.asarray(y, np.float64), -448.0, 448.0).astype(np.float32).astype(ml_dtypes.float8_e4m3fn).view(np.uint8)


def e4m3fn_values(b):
    return E4M3FN[b]


T, K, B, G, D = 2048, 2048, 512, 128, 80


def setup_inputs():
    s = mx_kscale(K)
    c = np.abs(np.random.standard_normal((T, K)))
    c = (c - c.mean(axis=0)) * np.exp(0.3 * np.random.standard_normal((T, 1)))
    weight = 1.0 / np.sqrt((c * c).sum(axis=1))
    lib = c * s
    lib_scale = (np.abs(lib).reshape(T, K // G, G).max(axis=2) / 448.0).astype(np.float32)
    lib_bytes = e4m3fn_bytes(lib / np.repeat(f64(lib_scale), G, axis=1))
    full = np.random.standard_normal((B, K + D)) ** 2
    return {"lib_bytes": lib_bytes,
            "lib_scale": lib_scale,
            "q": bf(full[:, :K] / s ** 2),
            "q_mod": bf(full[:, D:] / s ** 2),
            "row_weight": bf(weight)}


def reference(lib_bytes, lib_scale, q, q_mod, row_weight):
    lib = e4m3fn_values(lib_bytes) * np.repeat(f64(lib_scale), G, axis=1)
    lq = mxq(lib, 1, "e4m3")
    r = mxq(np.sqrt(f64(q)), 1, "e4m3")
    r_mod = mxq(np.sqrt(f64(q_mod)), 1, "e4m3")
    plain = lq @ r.T
    moved = lq @ r_mod.T
    return np.maximum(plain, moved) * f64(row_weight)[:, None]

@@ -1,0 +1,526 @@
+from contextlib import ExitStack
+
+import concourse.mybir as mybir
+from concourse.masks import make_identity
+
+FLOPS = 2 * 2048 * 2048 * 512 * 2
+
+F32 = mybir.dt.float32
+BF16 = mybir.dt.bfloat16
+U32 = mybir.dt.uint32
+U8 = mybir.dt.uint8
+FP8 = mybir.dt.float8_e4m3fn
+FP8X4 = mybir.dt.float8_e4m3fn_x4
+ACT = mybir.ActivationFunctionType
+ALU = mybir.AluOpType
+
+P = 128
+K = 2048
+NQ = 512
+PASSES = 4
+TILES = 16
+BLOCK = 128
+
+
+def tile_modified_spectrum_search_d1_kernel(tc, lib_bytes, lib_scale, q, q_mod, row_weight, out):
+    nc = tc.nc
+    lib_rows = lib_bytes.rearrange("(p i) k -> p i k", i=TILES)
+    out_rows = out.rearrange("(p i) b -> p i b", i=TILES)
+    with ExitStack() as ctx:
+        keep = ctx.enter_context(tc.tile_pool(name="keep", bufs=1))
+        bytes_pool = ctx.enter_context(tc.tile_pool(name="bytes_in", bufs=16))
+        raw_pool = ctx.enter_context(tc.tile_pool(name="raw", bufs=16))
+        work = ctx.enter_context(tc.tile_pool(name="work", bufs=3))
+        codes_pool = ctx.enter_context(tc.tile_pool(name="codes", bufs=16))
+        fin = ctx.enter_context(tc.tile_pool(name="fin", bufs=4))
+        xpsum = ctx.enter_context(tc.psum_pool(name="xpsum", bufs=4))
+        mpsum = ctx.enter_context(tc.psum_pool(name="mpsum", bufs=4))
+
+        ident = keep.tile([P, P], F32, name="ident")
+        make_identity(nc, ident[:])
+        warm = keep.tile([P, 8], F32, name="warm")
+        nc.vector.memset(warm[:], 1.0)
+        warm2 = keep.tile([P, 8], F32, name="warm2")
+        nc.scalar.activation(warm2[:], warm[:], ACT.Sqrt)
+
+        scale = keep.tile([P, TILES, 16], F32, name="scale")
+        wrow = keep.tile([P, TILES], BF16, name="wrow")
+        wcol = keep.tile([P, TILES], F32, name="wcol")
+
+        T = {}
+
+        def load_lq(c):
+            src = (q, q_mod)[c // 4]
+            g = c % 4
+            view = src.rearrange("(b p) k -> p b k", p=P)
+            for h in (0, 1):
+                t = raw_pool.tile([P, 2, 512], BF16, name="qraw", align_bytes=64)
+                nc.sync.dma_start(out=t[:], in_=view[:, 2 * h : 2 * h + 2, 512 * g : 512 * g + 512])
+                T["LQ", c, h] = t
+
+        def load_sc():
+            nc.sync.dma_start(out=scale[:], in_=lib_scale.rearrange("(p i) j -> p i j", i=TILES))
+            nc.sync.dma_start(out=wrow[:], in_=row_weight.rearrange("(p i) -> p i", i=TILES))
+            nc.vector.tensor_copy(out=wcol[:], in_=wrow[:])
+
+        def load_l(i, n):
+            t = bytes_pool.tile([P, n, K], U8, name="libbytes", tag="libbytes%d" % n, align_bytes=64)
+            nc.sync.dma_start(out=t[:], in_=lib_rows[:, i : i + n, :])
+            for d in range(n):
+                T["L", i + d] = t[:, d, :]
+
+        def widen(i, h):
+            if h == 0:
+                T["W", i] = work.tile([P, PASSES, 2, P, 2], BF16, name="wide", align_bytes=64)
+            wide = T["W", i]
+            for j in range(8 * h, 8 * h + 8):
+                g, s = j // 4, j % 4
+                nc.vector.tensor_scalar(
+                    out=wide[:, g, :, 32 * s : 32 * s + 32, :].rearrange("p u w e -> p w u e"),
+                    in0=T["L", i][:, BLOCK * j : BLOCK * j + BLOCK].bitcast(FP8).rearrange("p (w u e) -> p w u e", u=2, e=2),
+                    scalar1=scale[:, i, j : j + 1],
+                    scalar2=None,
+                    op0=ALU.mult,
+                )
+
+        def lib_x(i, h):
+            bank = xpsum.tile([P, 2, 2, P], F32, name="xbank")
+            words = T["W", i][:].rearrange("p g u w e -> p (g u w e)").bitcast(F32)
+            for gg in (0, 1):
+                for u in (0, 1):
+                    c0 = 256 * (2 * h + gg) + 128 * u
+                    nc.tensor.transpose(bank[:, u, gg, :], words[:, c0 : c0 + 128], ident[:])
+            T["X", i, h] = bank
+
+        def lib_c(i, h, eng):
+            if ("G", i) not in T:
+                T["G", i] = work.tile([P, 2048], BF16, name="grouped", align_bytes=64)
+            bank = T["X", i, h]
+            dst = T["G", i][:, 1024 * h : 1024 * h + 1024].bitcast(F32).rearrange("p (r u) -> p r u", u=2)
+            srcv = bank[:].rearrange("p u g r -> p (g r) u")
+            if eng == "V":
+                nc.vector.tensor_copy(out=dst, in_=srcv)
+            else:
+                nc.scalar.copy(dst, srcv)
+
+        def lib_z(i):
+            codes = codes_pool.tile([P, PASSES * P], U32, name="lcodes", align_bytes=64)
+            planes = codes_pool.tile([P, PASSES * P], U8, name="lplanes", align_bytes=64)
+            nc.vector.quantize_mx(out=codes[:].bitcast(FP8X4), scales=planes[:], in_=T["G", i][:])
+            T["Z", i] = (codes, planes)
+
+        def q_x(c, h):
+            bank = xpsum.tile([P, 2, 2, P], F32, name="xbank")
+            words = T["LQ", c, h][:].rearrange("p b k -> p (b k)").bitcast(F32)
+            for bb in (0, 1):
+                for u in (0, 1):
+                    nc.tensor.transpose(bank[:, u, bb, :], words[:, 256 * bb + u : 256 * bb + 256 : 2], ident[:])
+            T["QX", c, h] = bank
+
+        def q_a(c, h):
+            if h == 0 or ("QG", c) not in T:
+                T["QG", c] = work.tile([P, 2048], BF16, name="qroot", align_bytes=64)
+            bank = T["QX", c, h]
+            nc.scalar.activation(
+                T["QG", c][:, 1024 * h : 1024 * h + 1024].rearrange("p (r u e) -> p r u e", u=2, e=2),
+                bank[:].rearrange("p u b r -> p (u b r)").bitcast(BF16).rearrange("p (u r e) -> p r u e", u=2, e=2),
+                ACT.Sqrt,
+            )
+
+        def q_z(c):
+            codes = keep.tile([P, NQ], U32, name="qcodes%d" % c, align_bytes=64)
+            planes = keep.tile([P, NQ], U8, name="qplanes%d" % c, align_bytes=64)
+            nc.vector.quantize_mx(out=codes[:].bitcast(FP8X4), scales=planes[:], in_=T["QG", c][:])
+            T["QZ", c] = (codes, planes)
+
+        def mm(kind, i, g):
+            if g == 0:
+                T[kind, i] = mpsum.tile([P, NQ], F32, name="mbank")
+            c = g + (4 if kind == "M" else 0)
+            lc, lp = T["Z", i]
+            qc, qp = T["QZ", c]
+            nc.tensor.matmul_mx(
+                out=T[kind, i][:],
+                lhsT=lc[:, P * g : P * g + P].bitcast(FP8X4),
+                lhsT_scale=lp[:, P * g : P * g + P],
+                rhs=qc[:].bitcast(FP8X4),
+                rhs_scale=qp[:],
+                start=(g == 0),
+                stop=(g == PASSES - 1),
+            )
+
+        def e_p(i, eng):
+            t = fin.tile([P, NQ], F32, name="plain", bufs=8)
+            if eng == "V":
+                nc.vector.tensor_copy(out=t[:], in_=T["P", i][:])
+            else:
+                nc.scalar.copy(t[:], T["P", i][:])
+            T["EP", i] = t
+
+        def e_m(i):
+            t = fin.tile([P, NQ], F32, name="better")
+            nc.vector.tensor_tensor(out=t[:], in0=T["M", i][:], in1=T["EP", i][:], op=ALU.max)
+            T["EM", i] = t
+
+        def fin_w(i, eng):
+            t = fin.tile([P, NQ], F32, name="result")
+            if eng == "V":
+                nc.vector.tensor_scalar(out=t[:], in0=T["EM", i][:], scalar1=wcol[:, i : i + 1], scalar2=None, op0=ALU.mult)
+            else:
+                nc.scalar.activation(t[:], T["EM", i][:], ACT.Copy, scale=wcol[:, i : i + 1])
+            nc.sync.dma_start(out=out_rows[:, i, :], in_=t[:])
+
+        with tc.manual_schedule():
+            load_lq(0)
+            load_sc()
+            load_l(0, 1)
+            load_lq(1)
+            load_l(1, 1)
+            load_lq(2)
+            load_l(2, 1)
+            load_lq(3)
+            load_l(3, 1)
+            load_lq(4)
+            load_l(4, 1)
+            load_lq(5)
+            load_l(5, 1)
+            load_lq(6)
+            load_l(6, 1)
+            load_lq(7)
+            load_l(7, 1)
+            load_l(8, 1)
+            load_l(9, 1)
+            load_l(10, 1)
+            load_l(11, 1)
+            load_l(12, 1)
+            load_l(13, 1)
+            load_l(14, 1)
+            load_l(15, 1)
+            q_x(0, 0)
+            q_x(0, 1)
+            q_a(0, 0)
+            widen(0, 0)
+            q_a(0, 1)
+            widen(0, 1)
+            lib_x(0, 0)
+            q_x(1, 0)
+            lib_c(0, 0, "V")
+            lib_x(0, 1)
+            q_a(1, 0)
+            q_z(0)
+            q_x(1, 1)
+            lib_c(0, 1, "V")
+            q_x(2, 0)
+            q_a(1, 1)
+            widen(1, 0)
+            q_x(2, 1)
+            lib_z(0)
+            lib_x(1, 0)
+            q_a(2, 0)
+            q_z(1)
+            q_x(3, 0)
+            mm("P", 0, 0)
+            widen(1, 1)
+            q_a(3, 0)
+            mm("P", 0, 1)
+            q_x(3, 1)
+            lib_c(1, 0, "V")
+            widen(3, 0)
+            q_a(2, 1)
+            lib_x(1, 1)
+            q_x(4, 0)
+            lib_c(1, 1, "V")
+            q_a(3, 1)
+            q_z(2)
+            q_x(4, 1)
+            lib_x(3, 0)
+            lib_z(1)
+            mm("P", 0, 2)
+            lib_c(3, 0, "S")
+            q_z(3)
+            mm("P", 1, 0)
+            q_a(4, 0)
+            mm("P", 1, 1)
+            widen(3, 1)
+            mm("P", 0, 3)
+            mm("P", 1, 2)
+            e_p(0, "V")
+            mm("P", 1, 3)
+            q_a(4, 1)
+            lib_x(3, 1)
+            e_p(1, "V")
+            q_x(5, 0)
+            lib_c(3, 1, "V")
+            q_x(5, 1)
+            q_a(5, 0)
+            q_z(4)
+            q_x(6, 0)
+            lib_z(3)
+            mm("M", 1, 0)
+            q_a(5, 1)
+            mm("M", 0, 0)
+            widen(4, 0)
+            mm("P", 3, 0)
+            mm("P", 3, 1)
+            widen(4, 1)
+            q_a(6, 0)
+            mm("P", 3, 2)
+            mm("P", 3, 3)
+            lib_x(4, 0)
+            q_z(5)
+            lib_x(4, 1)
+            e_p(3, "S")
+            widen(2, 0)
+            mm("M", 1, 1)
+            lib_c(4, 0, "S")
+            mm("M", 0, 1)
+            widen(2, 1)
+            lib_x(2, 0)
+            lib_c(4, 1, "S")
+            q_x(6, 1)
+            widen(5, 0)
+            lib_c(2, 0, "S")
+            lib_x(2, 1)
+            widen(5, 1)
+            q_a(6, 1)
+            lib_x(5, 0)
+            q_x(7, 0)
+            lib_c(5, 0, "V")
+            mm("M", 3, 0)
+            lib_c(2, 1, "S")
+            q_z(6)
+            lib_x(5, 1)
+            q_a(7, 0)
+            q_x(7, 1)
+            lib_z(2)
+            mm("M", 1, 2)
+            lib_c(5, 1, "V")
+            q_a(7, 1)
+            mm("P", 2, 0)
+            lib_z(4)
+            mm("P", 2, 1)
+            mm("P", 2, 2)
+            lib_z(5)
+            mm("P", 2, 3)
+            mm("M", 0, 2)
+            e_p(2, "S")
+            q_z(7)
+            mm("M", 3, 1)
+            mm("M", 3, 2)
+            widen(7, 0)
+            mm("M", 2, 0)
+            mm("M", 2, 1)
+            mm("M", 2, 2)
+            widen(7, 1)
+            mm("M", 2, 3)
+            mm("M", 1, 3)
+            e_m(2)
+            mm("M", 0, 3)
+            mm("M", 3, 3)
+            e_m(1)
+            lib_x(7, 0)
+            fin_w(2, "S")
+            mm("P", 4, 0)
+            e_m(3)
+            fin_w(1, "S")
+            mm("P", 4, 1)
+            e_m(0)
+            mm("P", 4, 2)
+            fin_w(3, "S")
+            mm("P", 4, 3)
+            widen(8, 0)
+            mm("P", 5, 0)
+            e_p(4, "S")
+            mm("P", 5, 1)
+            mm("P", 5, 2)
+            widen(8, 1)
+            fin_w(0, "S")
+            mm("P", 5, 3)
+            mm("M", 5, 0)
+            e_p(5, "S")
+            widen(6, 0)
+            mm("M", 5, 1)
+            mm("M", 5, 2)
+            lib_c(7, 0, "S")
+            mm("M", 5, 3)
+            widen(6, 1)
+            lib_x(6, 0)
+            lib_x(8, 0)
+            widen(14, 0)
+            lib_c(6, 0, "S")
+            lib_x(6, 1)
+            lib_x(8, 1)
+            widen(14, 1)
+            lib_c(8, 0, "S")
+            mm("M", 4, 0)
+            lib_c(6, 1, "S")
+            widen(10, 0)
+            mm("M", 4, 1)
+            mm("M", 4, 2)
+            lib_c(8, 1, "S")
+            mm("M", 4, 3)
+            lib_z(6)
+            lib_x(10, 0)
+            lib_z(8)
+            lib_x(7, 1)
+            lib_c(10, 0, "S")
+            mm("P", 6, 0)
+            e_m(4)
+            lib_c(7, 1, "S")
+            mm("P", 6, 1)
+            mm("P", 6, 2)
+            widen(10, 1)
+            fin_w(4, "S")
+            mm("P", 6, 3)
+            mm("M", 6, 0)
+            lib_z(7)
+            e_p(6, "S")
+            mm("M", 6, 1)
+            mm("M", 6, 2)
+            widen(9, 0)
+            mm("M", 6, 3)
+            mm("P", 7, 0)
+            mm("P", 7, 1)
+            e_m(6)
+            mm("P", 7, 2)
+            mm("P", 7, 3)
+            widen(9, 1)
+            fin_w(6, "S")
+            mm("M", 8, 0)
+            mm("M", 8, 1)
+            e_p(7, "V")
+            mm("M", 8, 2)
+            mm("M", 8, 3)
+            widen(11, 0)
+            lib_x(10, 1)
+            mm("P", 8, 0)
+            lib_c(10, 1, "S")
+            widen(11, 1)
+            mm("P", 8, 1)
+            mm("P", 8, 2)
+            widen(12, 0)
+            mm("P", 8, 3)
+            lib_x(9, 0)
+            e_p(8, "S")
+            widen(12, 1)
+            lib_x(9, 1)
+            lib_c(9, 0, "S")
+            lib_x(11, 0)
+            lib_c(9, 1, "V")
+            lib_x(11, 1)
+            lib_c(11, 0, "S")
+            lib_x(14, 0)
+            lib_c(11, 1, "V")
+            lib_x(14, 1)
+            lib_c(14, 0, "S")
+            lib_x(12, 0)
+            lib_z(9)
+            lib_x(12, 1)
+            lib_c(14, 1, "S")
+            e_m(8)
+            mm("M", 7, 0)
+            lib_c(12, 0, "S")
+            mm("P", 9, 0)
+            lib_z(14)
+            mm("P", 9, 1)
+            fin_w(8, "S")
+            mm("P", 9, 2)
+            lib_z(10)
+            mm("P", 9, 3)
+            lib_c(12, 1, "S")
+            mm("M", 9, 0)
+            lib_z(11)
+            mm("M", 9, 1)
+            e_p(9, "S")
+            mm("M", 9, 2)
+            lib_z(12)
+            mm("M", 9, 3)
+            mm("P", 10, 0)
+            e_m(9)
+            mm("P", 10, 1)
+            mm("P", 10, 2)
+            e_m(5)
+            mm("P", 10, 3)
+            fin_w(9, "S")
+            mm("M", 12, 0)
+            e_p(10, "V")
+            mm("M", 12, 1)
+            fin_w(5, "S")
+            mm("M", 12, 2)
+            widen(13, 0)
+            mm("M", 12, 3)
+            mm("P", 12, 0)
+            mm("P", 12, 1)
+            widen(13, 1)
+            mm("P", 12, 2)
+            mm("P", 12, 3)
+            widen(15, 0)
+            mm("M", 10, 0)
+            e_p(12, "S")
+            mm("M", 10, 1)
+            mm("M", 10, 2)
+            widen(15, 1)
+            mm("M", 10, 3)
+            mm("P", 11, 0)
+            e_m(10)
+            mm("P", 11, 1)
+            mm("P", 11, 2)
+            e_m(12)
+            mm("P", 11, 3)
+            fin_w(10, "S")
+            mm("M", 11, 0)
+            e_p(11, "V")
+            mm("M", 11, 1)
+            fin_w(12, "S")
+            mm("M", 11, 2)
+            mm("M", 11, 3)
+            lib_x(15, 0)
+            e_m(11)
+            lib_x(15, 1)
+            lib_c(15, 0, "S")
+            lib_x(13, 0)
+            fin_w(11, "V")
+            lib_x(13, 1)
+            lib_c(15, 1, "S")
+            lib_c(13, 0, "V")
+            mm("P", 14, 0)
+            lib_c(13, 1, "S")
+            mm("P", 14, 1)
+            lib_z(15)
+            mm("P", 14, 2)
+            mm("P", 14, 3)
+            lib_z(13)
+            mm("P", 15, 0)
+            e_p(14, "S")
+            mm("P", 15, 1)
+            mm("P", 13, 0)
+            mm("P", 13, 1)
+            mm("P", 13, 2)
+            mm("P", 13, 3)
+            mm("M", 13, 0)
+            e_p(13, "S")
+            mm("M", 13, 1)
+            mm("M", 13, 2)
+            mm("M", 13, 3)
+            mm("P", 15, 2)
+            e_m(13)
+            mm("P", 15, 3)
+            mm("M", 7, 1)
+            e_p(15, "S")
+            mm("M", 7, 2)
+            fin_w(13, "V")
+            mm("M", 7, 3)
+            mm("M", 15, 0)
+            e_m(7)
+            mm("M", 15, 1)
+            mm("M", 15, 2)
+            mm("M", 15, 3)
+            fin_w(7, "S")
+            mm("M", 14, 0)
+            e_m(15)
+            mm("M", 14, 1)
+            mm("M", 14, 2)
+            mm("M", 14, 3)
+            fin_w(15, "S")
+            e_m(14)
+            fin_w(14, "S")

@@ -33,8 +33,8 @@ def tile_modified_spectrum_search_d1_kernel(tc, lib_bytes, lib_scale, q, q_mod, 
         work = ctx.enter_context(tc.tile_pool(name="work", bufs=3))
         codes_pool = ctx.enter_context(tc.tile_pool(name="codes", bufs=16))
         fin = ctx.enter_context(tc.tile_pool(name="fin", bufs=4))
-        xpsum = ctx.enter_context(tc.psum_pool(name="xpsum", bufs=4))
-        mpsum = ctx.enter_context(tc.psum_pool(name="mpsum", bufs=4))
+        xpsum = ctx.enter_context(tc.psum_pool(name="xpsum", bufs=5))
+        mpsum = ctx.enter_context(tc.psum_pool(name="mpsum", bufs=3))
 
         ident = keep.tile([P, P], F32, name="ident")
         make_identity(nc, ident[:])
@@ -202,320 +202,320 @@ def tile_modified_spectrum_search_d1_kernel(tc, lib_bytes, lib_scale, q, q_mod, 
             widen(0, 0)
             q_a(0, 1)
             widen(0, 1)
-            lib_x(0, 0)
             q_x(1, 0)
-            lib_c(0, 0, "V")
-            lib_x(0, 1)
-            q_a(1, 0)
+            lib_x(0, 0)
             q_z(0)
-            q_x(1, 1)
-            lib_c(0, 1, "V")
-            q_x(2, 0)
-            q_a(1, 1)
+            q_a(1, 0)
+            lib_x(0, 1)
             widen(1, 0)
-            q_x(2, 1)
-            lib_z(0)
+            lib_c(0, 0, "S")
+            q_x(1, 1)
+            widen(1, 1)
+            lib_c(0, 1, "S")
             lib_x(1, 0)
+            q_a(1, 1)
+            lib_z(0)
+            q_x(2, 0)
+            lib_c(1, 0, "V")
+            lib_x(1, 1)
             q_a(2, 0)
             q_z(1)
-            q_x(3, 0)
-            mm("P", 0, 0)
-            widen(1, 1)
-            q_a(3, 0)
-            mm("P", 0, 1)
-            q_x(3, 1)
-            lib_c(1, 0, "V")
-            widen(3, 0)
-            q_a(2, 1)
-            lib_x(1, 1)
-            q_x(4, 0)
+            q_x(2, 1)
             lib_c(1, 1, "V")
-            q_a(3, 1)
-            q_z(2)
-            q_x(4, 1)
-            lib_x(3, 0)
+            q_x(3, 0)
+            q_a(2, 1)
+            widen(2, 0)
+            q_x(3, 1)
             lib_z(1)
-            mm("P", 0, 2)
-            lib_c(3, 0, "S")
-            q_z(3)
+            q_a(3, 0)
+            q_x(4, 0)
+            q_z(2)
+            lib_x(2, 0)
+            q_a(3, 1)
+            widen(2, 1)
             mm("P", 1, 0)
+            widen(3, 0)
             q_a(4, 0)
             mm("P", 1, 1)
-            widen(3, 1)
-            mm("P", 0, 3)
             mm("P", 1, 2)
-            e_p(0, "V")
+            lib_x(2, 1)
+            q_z(3)
+            lib_c(2, 0, "S")
+            lib_x(3, 0)
+            widen(3, 1)
+            q_x(4, 1)
+            lib_c(2, 1, "S")
             mm("P", 1, 3)
+            lib_c(3, 0, "S")
+            widen(4, 0)
+            mm("P", 0, 0)
             q_a(4, 1)
             lib_x(3, 1)
-            e_p(1, "V")
-            q_x(5, 0)
-            lib_c(3, 1, "V")
-            q_x(5, 1)
-            q_a(5, 0)
-            q_z(4)
-            q_x(6, 0)
-            lib_z(3)
-            mm("M", 1, 0)
-            q_a(5, 1)
-            mm("M", 0, 0)
-            widen(4, 0)
-            mm("P", 3, 0)
-            mm("P", 3, 1)
-            widen(4, 1)
-            q_a(6, 0)
-            mm("P", 3, 2)
-            mm("P", 3, 3)
-            lib_x(4, 0)
-            q_z(5)
-            lib_x(4, 1)
-            e_p(3, "S")
-            widen(2, 0)
-            mm("M", 1, 1)
-            lib_c(4, 0, "S")
-            mm("M", 0, 1)
-            widen(2, 1)
-            lib_x(2, 0)
-            lib_c(4, 1, "S")
-            q_x(6, 1)
-            widen(5, 0)
-            lib_c(2, 0, "S")
-            lib_x(2, 1)
-            widen(5, 1)
-            q_a(6, 1)
-            lib_x(5, 0)
-            q_x(7, 0)
-            lib_c(5, 0, "V")
-            mm("M", 3, 0)
-            lib_c(2, 1, "S")
-            q_z(6)
-            lib_x(5, 1)
-            q_a(7, 0)
-            q_x(7, 1)
+            mm("P", 0, 1)
             lib_z(2)
-            mm("M", 1, 2)
-            lib_c(5, 1, "V")
-            q_a(7, 1)
+            mm("P", 0, 2)
+            lib_c(3, 1, "S")
+            widen(4, 1)
+            mm("P", 0, 3)
             mm("P", 2, 0)
-            lib_z(4)
+            e_p(1, "S")
             mm("P", 2, 1)
             mm("P", 2, 2)
-            lib_z(5)
+            q_z(4)
+            e_p(0, "S")
             mm("P", 2, 3)
-            mm("M", 0, 2)
+            q_x(5, 0)
+            widen(5, 0)
             e_p(2, "S")
+            mm("M", 0, 0)
+            q_a(5, 0)
+            widen(5, 1)
+            mm("M", 1, 0)
+            mm("M", 2, 0)
+            lib_x(5, 0)
+            lib_z(3)
+            q_x(5, 1)
+            lib_c(5, 0, "S")
+            widen(6, 0)
+            lib_x(5, 1)
+            q_a(5, 1)
+            lib_x(4, 0)
+            lib_x(4, 1)
+            lib_c(5, 1, "V")
+            q_x(6, 0)
+            lib_c(4, 0, "S")
+            widen(6, 1)
+            lib_x(6, 0)
+            lib_c(4, 1, "S")
+            q_x(6, 1)
+            lib_z(5)
+            q_a(6, 0)
+            lib_z(4)
+            lib_x(6, 1)
+            q_a(6, 1)
+            q_z(5)
+            q_x(7, 0)
+            widen(9, 0)
+            q_x(7, 1)
+            q_a(7, 0)
+            mm("M", 0, 1)
+            q_z(6)
+            q_a(7, 1)
+            widen(9, 1)
+            mm("M", 1, 1)
+            mm("M", 0, 2)
+            mm("M", 1, 2)
+            widen(10, 0)
+            lib_c(6, 0, "S")
+            mm("M", 2, 1)
+            mm("M", 2, 2)
+            lib_c(6, 1, "S")
+            lib_x(9, 0)
             q_z(7)
+            lib_x(9, 1)
+            lib_c(9, 0, "S")
+            lib_z(6)
+            lib_x(10, 0)
+            mm("M", 0, 3)
+            lib_c(9, 1, "S")
+            widen(10, 1)
+            mm("M", 1, 3)
+            lib_c(10, 0, "S")
+            mm("M", 2, 3)
+            e_m(0)
+            lib_x(10, 1)
+            e_m(1)
+            fin_w(0, "S")
+            mm("P", 5, 0)
+            e_m(2)
+            mm("P", 5, 1)
+            lib_c(10, 1, "S")
+            mm("P", 5, 2)
+            fin_w(1, "V")
+            mm("P", 5, 3)
+            fin_w(2, "S")
+            widen(8, 0)
+            mm("M", 4, 0)
+            mm("M", 4, 1)
+            e_p(5, "S")
+            mm("M", 4, 2)
+            mm("M", 4, 3)
+            widen(8, 1)
+            mm("M", 3, 0)
             mm("M", 3, 1)
             mm("M", 3, 2)
             widen(7, 0)
-            mm("M", 2, 0)
-            mm("M", 2, 1)
-            mm("M", 2, 2)
-            widen(7, 1)
-            mm("M", 2, 3)
-            mm("M", 1, 3)
-            e_m(2)
-            mm("M", 0, 3)
             mm("M", 3, 3)
-            e_m(1)
-            lib_x(7, 0)
-            fin_w(2, "S")
-            mm("P", 4, 0)
-            e_m(3)
-            fin_w(1, "S")
-            mm("P", 4, 1)
-            e_m(0)
-            mm("P", 4, 2)
-            fin_w(3, "S")
-            mm("P", 4, 3)
-            widen(8, 0)
-            mm("P", 5, 0)
-            e_p(4, "S")
-            mm("P", 5, 1)
-            mm("P", 5, 2)
-            widen(8, 1)
-            fin_w(0, "S")
-            mm("P", 5, 3)
-            mm("M", 5, 0)
-            e_p(5, "S")
-            widen(6, 0)
-            mm("M", 5, 1)
-            mm("M", 5, 2)
-            lib_c(7, 0, "S")
-            mm("M", 5, 3)
-            widen(6, 1)
-            lib_x(6, 0)
+            mm("P", 3, 0)
+            mm("P", 3, 1)
+            widen(7, 1)
+            mm("P", 3, 2)
+            mm("P", 3, 3)
             lib_x(8, 0)
-            widen(14, 0)
-            lib_c(6, 0, "S")
-            lib_x(6, 1)
-            lib_x(8, 1)
-            widen(14, 1)
-            lib_c(8, 0, "S")
-            mm("M", 4, 0)
-            lib_c(6, 1, "S")
-            widen(10, 0)
-            mm("M", 4, 1)
-            mm("M", 4, 2)
-            lib_c(8, 1, "S")
-            mm("M", 4, 3)
-            lib_z(6)
-            lib_x(10, 0)
-            lib_z(8)
-            lib_x(7, 1)
-            lib_c(10, 0, "S")
-            mm("P", 6, 0)
-            e_m(4)
-            lib_c(7, 1, "S")
-            mm("P", 6, 1)
-            mm("P", 6, 2)
-            widen(10, 1)
-            fin_w(4, "S")
-            mm("P", 6, 3)
-            mm("M", 6, 0)
-            lib_z(7)
-            e_p(6, "S")
-            mm("M", 6, 1)
-            mm("M", 6, 2)
-            widen(9, 0)
-            mm("M", 6, 3)
-            mm("P", 7, 0)
-            mm("P", 7, 1)
-            e_m(6)
-            mm("P", 7, 2)
-            mm("P", 7, 3)
-            widen(9, 1)
-            fin_w(6, "S")
-            mm("M", 8, 0)
-            mm("M", 8, 1)
-            e_p(7, "V")
-            mm("M", 8, 2)
-            mm("M", 8, 3)
-            widen(11, 0)
-            lib_x(10, 1)
-            mm("P", 8, 0)
-            lib_c(10, 1, "S")
-            widen(11, 1)
-            mm("P", 8, 1)
-            mm("P", 8, 2)
-            widen(12, 0)
-            mm("P", 8, 3)
-            lib_x(9, 0)
-            e_p(8, "S")
-            widen(12, 1)
-            lib_x(9, 1)
-            lib_c(9, 0, "S")
-            lib_x(11, 0)
-            lib_c(9, 1, "V")
-            lib_x(11, 1)
-            lib_c(11, 0, "S")
-            lib_x(14, 0)
-            lib_c(11, 1, "V")
-            lib_x(14, 1)
-            lib_c(14, 0, "S")
-            lib_x(12, 0)
-            lib_z(9)
-            lib_x(12, 1)
-            lib_c(14, 1, "S")
-            e_m(8)
-            mm("M", 7, 0)
-            lib_c(12, 0, "S")
-            mm("P", 9, 0)
-            lib_z(14)
-            mm("P", 9, 1)
-            fin_w(8, "S")
-            mm("P", 9, 2)
+            e_p(3, "S")
             lib_z(10)
-            mm("P", 9, 3)
-            lib_c(12, 1, "S")
-            mm("M", 9, 0)
-            lib_z(11)
-            mm("M", 9, 1)
-            e_p(9, "S")
-            mm("M", 9, 2)
-            lib_z(12)
-            mm("M", 9, 3)
+            lib_x(8, 1)
+            lib_c(8, 0, "S")
+            lib_x(7, 0)
+            lib_z(9)
+            mm("P", 4, 0)
+            lib_c(8, 1, "S")
+            e_m(3)
+            mm("P", 4, 1)
+            mm("P", 4, 2)
+            lib_c(7, 0, "S")
+            widen(11, 0)
+            mm("P", 4, 3)
             mm("P", 10, 0)
-            e_m(9)
+            fin_w(3, "S")
             mm("P", 10, 1)
             mm("P", 10, 2)
-            e_m(5)
+            e_p(4, "S")
+            lib_z(8)
             mm("P", 10, 3)
-            fin_w(9, "S")
-            mm("M", 12, 0)
-            e_p(10, "V")
-            mm("M", 12, 1)
-            fin_w(5, "S")
-            mm("M", 12, 2)
+            lib_x(11, 0)
+            widen(11, 1)
+            e_p(10, "S")
+            mm("P", 8, 0)
+            lib_c(11, 0, "S")
+            mm("P", 8, 1)
+            widen(12, 0)
+            mm("P", 8, 2)
+            mm("P", 8, 3)
+            mm("M", 5, 0)
+            e_p(8, "S")
+            mm("M", 5, 1)
+            widen(12, 1)
+            mm("M", 5, 2)
+            mm("M", 5, 3)
+            lib_x(11, 1)
             widen(13, 0)
-            mm("M", 12, 3)
-            mm("P", 12, 0)
-            mm("P", 12, 1)
+            lib_x(12, 0)
+            lib_c(11, 1, "S")
+            lib_x(12, 1)
+            e_m(5)
+            mm("M", 6, 0)
+            lib_c(12, 0, "S")
+            mm("M", 6, 1)
+            lib_z(11)
+            lib_c(12, 1, "S")
+            mm("M", 6, 2)
+            mm("M", 6, 3)
+            fin_w(5, "V")
+            mm("P", 6, 0)
             widen(13, 1)
-            mm("P", 12, 2)
-            mm("P", 12, 3)
-            widen(15, 0)
-            mm("M", 10, 0)
-            e_p(12, "S")
-            mm("M", 10, 1)
-            mm("M", 10, 2)
-            widen(15, 1)
-            mm("M", 10, 3)
-            mm("P", 11, 0)
-            e_m(10)
-            mm("P", 11, 1)
-            mm("P", 11, 2)
-            e_m(12)
-            mm("P", 11, 3)
-            fin_w(10, "S")
-            mm("M", 11, 0)
-            e_p(11, "V")
-            mm("M", 11, 1)
-            fin_w(12, "S")
-            mm("M", 11, 2)
-            mm("M", 11, 3)
-            lib_x(15, 0)
-            e_m(11)
-            lib_x(15, 1)
-            lib_c(15, 0, "S")
+            mm("P", 6, 1)
+            mm("P", 6, 2)
+            mm("P", 6, 3)
+            lib_z(12)
+            lib_x(7, 1)
+            e_p(6, "S")
             lib_x(13, 0)
-            fin_w(11, "V")
+            e_m(4)
+            lib_c(7, 1, "S")
             lib_x(13, 1)
-            lib_c(15, 1, "S")
+            e_m(6)
+            mm("M", 12, 0)
+            fin_w(4, "S")
+            mm("M", 12, 1)
+            lib_z(7)
+            mm("M", 12, 2)
+            fin_w(6, "S")
+            mm("M", 12, 3)
             lib_c(13, 0, "V")
-            mm("P", 14, 0)
+            mm("P", 12, 0)
             lib_c(13, 1, "S")
-            mm("P", 14, 1)
-            lib_z(15)
-            mm("P", 14, 2)
-            mm("P", 14, 3)
+            mm("P", 7, 0)
+            widen(14, 0)
+            mm("P", 7, 1)
+            mm("P", 7, 2)
+            mm("P", 7, 3)
             lib_z(13)
-            mm("P", 15, 0)
-            e_p(14, "S")
-            mm("P", 15, 1)
+            mm("P", 12, 1)
+            e_p(7, "S")
+            mm("P", 12, 2)
+            widen(14, 1)
+            mm("P", 12, 3)
+            lib_x(14, 0)
+            e_p(12, "S")
+            mm("M", 7, 0)
+            widen(15, 0)
+            lib_c(14, 0, "S")
+            mm("M", 7, 1)
+            mm("M", 7, 2)
+            mm("M", 7, 3)
+            e_m(12)
             mm("P", 13, 0)
             mm("P", 13, 1)
+            e_m(7)
             mm("P", 13, 2)
+            fin_w(12, "S")
             mm("P", 13, 3)
-            mm("M", 13, 0)
+            widen(15, 1)
+            mm("P", 11, 0)
+            fin_w(7, "S")
+            mm("P", 11, 1)
+            mm("P", 11, 2)
             e_p(13, "S")
+            mm("P", 11, 3)
+            lib_x(14, 1)
+            e_p(11, "S")
+            lib_x(15, 0)
+            lib_c(14, 1, "V")
+            lib_x(15, 1)
+            lib_c(15, 0, "S")
+            mm("M", 8, 0)
+            lib_c(15, 1, "V")
+            mm("M", 8, 1)
+            mm("M", 8, 2)
+            lib_z(14)
+            mm("M", 8, 3)
+            mm("P", 9, 0)
+            lib_z(15)
+            mm("P", 9, 1)
+            mm("P", 9, 2)
+            e_m(8)
+            mm("P", 9, 3)
+            mm("P", 15, 0)
+            e_p(9, "S")
+            mm("P", 15, 1)
+            fin_w(8, "V")
+            mm("P", 15, 2)
+            mm("P", 15, 3)
+            mm("M", 10, 0)
+            e_p(15, "S")
+            mm("M", 10, 1)
+            mm("M", 10, 2)
+            mm("M", 10, 3)
+            mm("M", 9, 0)
+            e_m(10)
+            mm("M", 9, 1)
+            mm("M", 9, 2)
+            mm("M", 9, 3)
+            fin_w(10, "S")
+            mm("P", 14, 0)
+            e_m(9)
+            mm("P", 14, 1)
+            mm("P", 14, 2)
+            mm("P", 14, 3)
+            fin_w(9, "S")
+            mm("M", 13, 0)
+            e_p(14, "V")
             mm("M", 13, 1)
             mm("M", 13, 2)
             mm("M", 13, 3)
-            mm("P", 15, 2)
+            mm("M", 11, 0)
             e_m(13)
-            mm("P", 15, 3)
-            mm("M", 7, 1)
-            e_p(15, "S")
-            mm("M", 7, 2)
-            fin_w(13, "V")
-            mm("M", 7, 3)
+            mm("M", 11, 1)
+            mm("M", 11, 2)
+            mm("M", 11, 3)
+            fin_w(13, "S")
             mm("M", 15, 0)
-            e_m(7)
+            e_m(11)
             mm("M", 15, 1)
             mm("M", 15, 2)
             mm("M", 15, 3)
-            fin_w(7, "S")
+            fin_w(11, "S")
             mm("M", 14, 0)
             e_m(15)
             mm("M", 14, 1)

@@ -3,7 +3,7 @@ from contextlib import ExitStack
 import concourse.mybir as mybir
 from concourse.masks import make_identity
 
-FLOPS = 2 * 2048 * 2048 * 512 * 2
+FLOPS = 2 * 2 * 2048 * 512 * 2048
 
 F32 = mybir.dt.float32
 BF16 = mybir.dt.bfloat16
@@ -16,511 +16,269 @@ ALU = mybir.AluOpType
 
 P = 128
 K = 2048
-NQ = 512
-PASSES = 4
-TILES = 16
-BLOCK = 128
+QUERIES = 512
+K_PASS = 512
+PASSES = K // K_PASS
+TILES = 2048 // P
+HALVES = 2 * TILES
+CHUNKS = 2 * PASSES
+SCALE_K = 128
+SCALES = K // SCALE_K
+
+TURN_BANKS = 5
+PRODUCT_BANKS = 3
+
+WIDENED_BY_CHUNK = (2, 3, 4, 4, 4, 6, 9, 9)
+VECTOR_HALVES = 6
+STEP_TILES = 2
+WIDEN_AHEAD = 2
+LAST_PARTS = 2
 
 
 def tile_modified_spectrum_search_d1_kernel(tc, lib_bytes, lib_scale, q, q_mod, row_weight, out):
     nc = tc.nc
     lib_rows = lib_bytes.rearrange("(p i) k -> p i k", i=TILES)
     out_rows = out.rearrange("(p i) b -> p i b", i=TILES)
+
     with ExitStack() as ctx:
-        keep = ctx.enter_context(tc.tile_pool(name="keep", bufs=1))
-        bytes_pool = ctx.enter_context(tc.tile_pool(name="bytes_in", bufs=16))
-        raw_pool = ctx.enter_context(tc.tile_pool(name="raw", bufs=16))
-        work = ctx.enter_context(tc.tile_pool(name="work", bufs=3))
-        codes_pool = ctx.enter_context(tc.tile_pool(name="codes", bufs=16))
-        fin = ctx.enter_context(tc.tile_pool(name="fin", bufs=4))
-        xpsum = ctx.enter_context(tc.psum_pool(name="xpsum", bufs=5))
-        mpsum = ctx.enter_context(tc.psum_pool(name="mpsum", bufs=3))
+        const = ctx.enter_context(tc.tile_pool(name="const", bufs=1))
+        inputs = ctx.enter_context(tc.tile_pool(name="inputs", bufs=TILES))
+        work = ctx.enter_context(tc.tile_pool(name="work", bufs=4))
+        codes = ctx.enter_context(tc.tile_pool(name="codes", bufs=TILES))
+        ends = ctx.enter_context(tc.tile_pool(name="ends", bufs=6))
+        turn_psum = ctx.enter_context(tc.psum_pool(name="turn_psum", bufs=TURN_BANKS))
+        product_psum = ctx.enter_context(tc.psum_pool(name="product_psum", bufs=PRODUCT_BANKS))
 
-        ident = keep.tile([P, P], F32, name="ident")
+        ident = const.tile([P, P], F32, name="ident")
         make_identity(nc, ident[:])
-        warm = keep.tile([P, 8], F32, name="warm")
-        nc.vector.memset(warm[:], 1.0)
-        warm2 = keep.tile([P, 8], F32, name="warm2")
-        nc.scalar.activation(warm2[:], warm[:], ACT.Sqrt)
+        scale = const.tile([P, TILES, SCALES], F32, name="scale")
+        weight_in = const.tile([P, TILES], BF16, name="weight_in")
+        weight = const.tile([P, TILES], F32, name="weight")
 
-        scale = keep.tile([P, TILES, 16], F32, name="scale")
-        wrow = keep.tile([P, TILES], BF16, name="wrow")
-        wcol = keep.tile([P, TILES], F32, name="wcol")
+        raw_query, query_bank, roots, query_codes = {}, {}, {}, {}
+        lib_in, wide, lib_bank, grouped, lib_codes = {}, {}, {}, {}, {}
+        plain_bank, plain, moved_bank, better = {}, {}, {}, {}
+        done = {"widened": 0, "turned": 0, "copied": 0, "quantised": 0, "query_halves": 0, "root_halves": 0}
+        passes_done = {"plain": [0] * TILES, "moved": [0] * TILES}
+        weighed = set()
 
-        T = {}
-
-        def load_lq(c):
-            src = (q, q_mod)[c // 4]
-            g = c % 4
-            view = src.rearrange("(b p) k -> p b k", p=P)
+        def load_query(c):
+            source = (q if c < PASSES else q_mod).rearrange("(b p) k -> p b k", p=P)
+            k0 = K_PASS * (c % PASSES)
             for h in (0, 1):
-                t = raw_pool.tile([P, 2, 512], BF16, name="qraw", align_bytes=64)
-                nc.sync.dma_start(out=t[:], in_=view[:, 2 * h : 2 * h + 2, 512 * g : 512 * g + 512])
-                T["LQ", c, h] = t
+                raw = inputs.tile([P, 2, K_PASS], BF16, name="raw_query", align_bytes=64)
+                nc.sync.dma_start(out=raw[:], in_=source[:, 2 * h : 2 * h + 2, k0 : k0 + K_PASS])
+                raw_query[c, h] = raw
 
-        def load_sc():
-            nc.sync.dma_start(out=scale[:], in_=lib_scale.rearrange("(p i) j -> p i j", i=TILES))
-            nc.sync.dma_start(out=wrow[:], in_=row_weight.rearrange("(p i) -> p i", i=TILES))
-            nc.vector.tensor_copy(out=wcol[:], in_=wrow[:])
+        def load_lib(i):
+            bytes_in = inputs.tile([P, K], U8, name="bytes_in", align_bytes=64)
+            nc.sync.dma_start(out=bytes_in[:], in_=lib_rows[:, i, :])
+            lib_in[i] = bytes_in
 
-        def load_l(i, n):
-            t = bytes_pool.tile([P, n, K], U8, name="libbytes", tag="libbytes%d" % n, align_bytes=64)
-            nc.sync.dma_start(out=t[:], in_=lib_rows[:, i : i + n, :])
-            for d in range(n):
-                T["L", i + d] = t[:, d, :]
+        def turn_query(c):
+            for h in (0, 1):
+                bank = turn_psum.tile([P, 2, 2, P], F32, name="turn_bank")
+                pairs = raw_query[c, h][:].rearrange("p b k -> p (b k)").bitcast(F32)
+                for b in (0, 1):
+                    for u in (0, 1):
+                        first = 256 * b
+                        nc.tensor.transpose(bank[:, u, b, :], pairs[:, first + u : first + 256 : 2], ident[:])
+                query_bank[c, h] = bank
+                done["query_halves"] += 1
 
-        def widen(i, h):
-            if h == 0:
-                T["W", i] = work.tile([P, PASSES, 2, P, 2], BF16, name="wide", align_bytes=64)
-            wide = T["W", i]
-            for j in range(8 * h, 8 * h + 8):
-                g, s = j // 4, j % 4
-                nc.vector.tensor_scalar(
-                    out=wide[:, g, :, 32 * s : 32 * s + 32, :].rearrange("p u w e -> p w u e"),
-                    in0=T["L", i][:, BLOCK * j : BLOCK * j + BLOCK].bitcast(FP8).rearrange("p (w u e) -> p w u e", u=2, e=2),
-                    scalar1=scale[:, i, j : j + 1],
-                    scalar2=None,
-                    op0=ALU.mult,
+        def root_query(c):
+            roots[c] = work.tile([P, 4 * QUERIES], BF16, name="roots", align_bytes=64)
+            for h in (0, 1):
+                values = query_bank[c, h][:].rearrange("p u b r -> p (u b r)").bitcast(BF16)
+                nc.scalar.activation(
+                    roots[c][:, 1024 * h : 1024 * h + 1024].rearrange("p (r u e) -> p r u e", u=2, e=2),
+                    values.rearrange("p (u r e) -> p r u e", u=2, e=2),
+                    ACT.Sqrt,
                 )
+                done["root_halves"] += 1
 
-        def lib_x(i, h):
-            bank = xpsum.tile([P, 2, 2, P], F32, name="xbank")
-            words = T["W", i][:].rearrange("p g u w e -> p (g u w e)").bitcast(F32)
-            for gg in (0, 1):
-                for u in (0, 1):
-                    c0 = 256 * (2 * h + gg) + 128 * u
-                    nc.tensor.transpose(bank[:, u, gg, :], words[:, c0 : c0 + 128], ident[:])
-            T["X", i, h] = bank
+        def quantise_query(c):
+            words = const.tile([P, QUERIES], U32, name="query_words%d" % c, align_bytes=64)
+            planes = const.tile([P, QUERIES], U8, name="query_planes%d" % c, align_bytes=64)
+            nc.vector.quantize_mx(out=words[:].bitcast(FP8X4), scales=planes[:], in_=roots[c][:])
+            query_codes[c] = (words, planes)
 
-        def lib_c(i, h, eng):
-            if ("G", i) not in T:
-                T["G", i] = work.tile([P, 2048], BF16, name="grouped", align_bytes=64)
-            bank = T["X", i, h]
-            dst = T["G", i][:, 1024 * h : 1024 * h + 1024].bitcast(F32).rearrange("p (r u) -> p r u", u=2)
-            srcv = bank[:].rearrange("p u g r -> p (g r) u")
-            if eng == "V":
-                nc.vector.tensor_copy(out=dst, in_=srcv)
-            else:
-                nc.scalar.copy(dst, srcv)
+        def widen_up_to(halves):
+            while done["widened"] < min(halves, HALVES):
+                i, h = divmod(done["widened"], 2)
+                if h == 0:
+                    wide[i] = work.tile([P, PASSES, 2, P, 2], BF16, name="wide", align_bytes=64)
+                for j in range(8 * h, 8 * h + 8):
+                    g, part = divmod(j, 4)
+                    nc.vector.tensor_scalar(
+                        out=wide[i][:, g, :, 32 * part : 32 * part + 32, :].rearrange("p u w e -> p w u e"),
+                        in0=lib_in[i][:, SCALE_K * j : SCALE_K * j + SCALE_K]
+                        .bitcast(FP8)
+                        .rearrange("p (w u e) -> p w u e", u=2, e=2),
+                        scalar1=scale[:, i, j : j + 1],
+                        scalar2=None,
+                        op0=ALU.mult,
+                    )
+                done["widened"] += 1
 
-        def lib_z(i):
-            codes = codes_pool.tile([P, PASSES * P], U32, name="lcodes", align_bytes=64)
-            planes = codes_pool.tile([P, PASSES * P], U8, name="lplanes", align_bytes=64)
-            nc.vector.quantize_mx(out=codes[:].bitcast(FP8X4), scales=planes[:], in_=T["G", i][:])
-            T["Z", i] = (codes, planes)
+        def turn_lib():
+            while (
+                done["turned"] < done["widened"]
+                and done["turned"] + done["query_halves"] - done["copied"] - done["root_halves"] < TURN_BANKS
+            ):
+                i, h = divmod(done["turned"], 2)
+                bank = turn_psum.tile([P, 2, 2, P], F32, name="turn_bank")
+                pairs = wide[i][:].rearrange("p g u w e -> p (g u w e)").bitcast(F32)
+                for b in (0, 1):
+                    for u in (0, 1):
+                        first = 256 * (2 * h + b) + P * u
+                        nc.tensor.transpose(bank[:, u, b, :], pairs[:, first : first + P], ident[:])
+                lib_bank[i, h] = bank
+                done["turned"] += 1
 
-        def q_x(c, h):
-            bank = xpsum.tile([P, 2, 2, P], F32, name="xbank")
-            words = T["LQ", c, h][:].rearrange("p b k -> p (b k)").bitcast(F32)
-            for bb in (0, 1):
-                for u in (0, 1):
-                    nc.tensor.transpose(bank[:, u, bb, :], words[:, 256 * bb + u : 256 * bb + 256 : 2], ident[:])
-            T["QX", c, h] = bank
+        def copy_lib():
+            while done["copied"] < done["turned"]:
+                i, h = divmod(done["copied"], 2)
+                if h == 0:
+                    grouped[i] = work.tile([P, 4 * PASSES * P], BF16, name="grouped", align_bytes=64)
+                target = grouped[i][:, 1024 * h : 1024 * h + 1024].bitcast(F32).rearrange("p (r u) -> p r u", u=2)
+                source = lib_bank[i, h][:].rearrange("p u b r -> p (b r) u")
+                if done["copied"] < VECTOR_HALVES:
+                    nc.vector.tensor_copy(out=target, in_=source)
+                else:
+                    nc.scalar.copy(target, source)
+                done["copied"] += 1
 
-        def q_a(c, h):
-            if h == 0 or ("QG", c) not in T:
-                T["QG", c] = work.tile([P, 2048], BF16, name="qroot", align_bytes=64)
-            bank = T["QX", c, h]
-            nc.scalar.activation(
-                T["QG", c][:, 1024 * h : 1024 * h + 1024].rearrange("p (r u e) -> p r u e", u=2, e=2),
-                bank[:].rearrange("p u b r -> p (u b r)").bitcast(BF16).rearrange("p (u r e) -> p r u e", u=2, e=2),
-                ACT.Sqrt,
-            )
+        def quantise_lib():
+            while done["quantised"] < done["copied"] // 2:
+                i = done["quantised"]
+                words = codes.tile([P, PASSES * P], U32, name="lib_words", align_bytes=64)
+                planes = codes.tile([P, PASSES * P], U8, name="lib_planes", align_bytes=64)
+                nc.vector.quantize_mx(out=words[:].bitcast(FP8X4), scales=planes[:], in_=grouped[i][:])
+                lib_codes[i] = (words, planes)
+                done["quantised"] += 1
 
-        def q_z(c):
-            codes = keep.tile([P, NQ], U32, name="qcodes%d" % c, align_bytes=64)
-            planes = keep.tile([P, NQ], U8, name="qplanes%d" % c, align_bytes=64)
-            nc.vector.quantize_mx(out=codes[:].bitcast(FP8X4), scales=planes[:], in_=T["QG", c][:])
-            T["QZ", c] = (codes, planes)
+        def moved_columns(i):
+            parts = LAST_PARTS if i == TILES - 1 else 1
+            width = QUERIES // parts
+            return [slice(width * part, width * (part + 1)) for part in range(parts)]
 
-        def mm(kind, i, g):
-            if g == 0:
-                T[kind, i] = mpsum.tile([P, NQ], F32, name="mbank")
-            c = g + (4 if kind == "M" else 0)
-            lc, lp = T["Z", i]
-            qc, qp = T["QZ", c]
+        def multiply(bank, i, g, c, columns):
+            words, planes = lib_codes[i]
+            query_words, query_planes = query_codes[c]
             nc.tensor.matmul_mx(
-                out=T[kind, i][:],
-                lhsT=lc[:, P * g : P * g + P].bitcast(FP8X4),
-                lhsT_scale=lp[:, P * g : P * g + P],
-                rhs=qc[:].bitcast(FP8X4),
-                rhs_scale=qp[:],
+                out=bank,
+                lhsT=words[:, P * g : P * g + P].bitcast(FP8X4),
+                lhsT_scale=planes[:, P * g : P * g + P],
+                rhs=query_words[:, columns].bitcast(FP8X4),
+                rhs_scale=query_planes[:, columns],
                 start=(g == 0),
                 stop=(g == PASSES - 1),
             )
 
-        def e_p(i, eng):
-            t = fin.tile([P, NQ], F32, name="plain", bufs=8)
-            if eng == "V":
-                nc.vector.tensor_copy(out=t[:], in_=T["P", i][:])
-            else:
-                nc.scalar.copy(t[:], T["P", i][:])
-            T["EP", i] = t
+        def multiply_plain(tiles):
+            for i in tiles:
+                while passes_done["plain"][i] < PASSES and i < done["quantised"] and passes_done["plain"][i] in query_codes:
+                    g = passes_done["plain"][i]
+                    if g == 0:
+                        plain_bank[i] = product_psum.tile([P, QUERIES], F32, name="product_bank")
+                    multiply(plain_bank[i][:], i, g, g, slice(0, QUERIES))
+                    passes_done["plain"][i] += 1
 
-        def e_m(i):
-            t = fin.tile([P, NQ], F32, name="better")
-            nc.vector.tensor_tensor(out=t[:], in0=T["M", i][:], in1=T["EP", i][:], op=ALU.max)
-            T["EM", i] = t
+        def multiply_moved(tiles):
+            for i in tiles:
+                if i < done["quantised"]:
+                    first, last = passes_done["moved"][i], max(0, len(query_codes) - PASSES)
+                    for part, columns in enumerate(moved_columns(i)):
+                        for g in range(first, last):
+                            if g == 0:
+                                moved_bank[i, part] = product_psum.tile([P, QUERIES], F32, name="product_bank")
+                            width = columns.stop - columns.start
+                            multiply(moved_bank[i, part][:, 0:width], i, g, PASSES + g, columns)
+                    passes_done["moved"][i] = last
 
-        def fin_w(i, eng):
-            t = fin.tile([P, NQ], F32, name="result")
-            if eng == "V":
-                nc.vector.tensor_scalar(out=t[:], in0=T["EM", i][:], scalar1=wcol[:, i : i + 1], scalar2=None, op0=ALU.mult)
-            else:
-                nc.scalar.activation(t[:], T["EM", i][:], ACT.Copy, scale=wcol[:, i : i + 1])
-            nc.sync.dma_start(out=out_rows[:, i, :], in_=t[:])
+        def save_plain():
+            for i in range(TILES):
+                if passes_done["plain"][i] == PASSES and i not in plain:
+                    plain[i] = ends.tile([P, QUERIES], F32, name="plain")
+                    nc.scalar.copy(plain[i][:], plain_bank[i][:])
+
+        def take_better_part(i, part, columns):
+            if part == 0:
+                better[i] = ends.tile([P, QUERIES], F32, name="better")
+            width = columns.stop - columns.start
+            nc.vector.tensor_tensor(
+                out=better[i][:, columns],
+                in0=moved_bank[i, part][:, 0:width],
+                in1=plain[i][:, columns],
+                op=ALU.max,
+            )
+
+        def take_better():
+            for i in range(TILES - 1):
+                if passes_done["moved"][i] == PASSES and i in plain and i not in better:
+                    take_better_part(i, 0, slice(0, QUERIES))
+
+        def weigh():
+            for i in range(TILES - 1):
+                if i in better and i not in weighed:
+                    result = ends.tile([P, QUERIES], F32, name="result")
+                    nc.scalar.activation(result[:], better[i][:], ACT.Copy, scale=weight[:, i : i + 1])
+                    nc.sync.dma_start(out=out_rows[:, i, :], in_=result[:])
+                    weighed.add(i)
+
+        def finish_last():
+            i = TILES - 1
+            for part, columns in enumerate(moved_columns(i)):
+                take_better_part(i, part, columns)
+                result = ends.tile([P, QUERIES // LAST_PARTS], F32, name="last_result")
+                nc.vector.tensor_scalar(
+                    out=result[:], in0=better[i][:, columns], scalar1=weight[:, i : i + 1], scalar2=None, op0=ALU.mult
+                )
+                nc.sync.dma_start(out=out_rows[:, i, columns], in_=result[:])
 
         with tc.manual_schedule():
-            load_lq(0)
-            load_sc()
-            load_l(0, 1)
-            load_lq(1)
-            load_l(1, 1)
-            load_lq(2)
-            load_l(2, 1)
-            load_lq(3)
-            load_l(3, 1)
-            load_lq(4)
-            load_l(4, 1)
-            load_lq(5)
-            load_l(5, 1)
-            load_lq(6)
-            load_l(6, 1)
-            load_lq(7)
-            load_l(7, 1)
-            load_l(8, 1)
-            load_l(9, 1)
-            load_l(10, 1)
-            load_l(11, 1)
-            load_l(12, 1)
-            load_l(13, 1)
-            load_l(14, 1)
-            load_l(15, 1)
-            q_x(0, 0)
-            q_x(0, 1)
-            q_a(0, 0)
-            widen(0, 0)
-            q_a(0, 1)
-            widen(0, 1)
-            q_x(1, 0)
-            lib_x(0, 0)
-            q_z(0)
-            q_a(1, 0)
-            lib_x(0, 1)
-            widen(1, 0)
-            lib_c(0, 0, "S")
-            q_x(1, 1)
-            widen(1, 1)
-            lib_c(0, 1, "S")
-            lib_x(1, 0)
-            q_a(1, 1)
-            lib_z(0)
-            q_x(2, 0)
-            lib_c(1, 0, "V")
-            lib_x(1, 1)
-            q_a(2, 0)
-            q_z(1)
-            q_x(2, 1)
-            lib_c(1, 1, "V")
-            q_x(3, 0)
-            q_a(2, 1)
-            widen(2, 0)
-            q_x(3, 1)
-            lib_z(1)
-            q_a(3, 0)
-            q_x(4, 0)
-            q_z(2)
-            lib_x(2, 0)
-            q_a(3, 1)
-            widen(2, 1)
-            mm("P", 1, 0)
-            widen(3, 0)
-            q_a(4, 0)
-            mm("P", 1, 1)
-            mm("P", 1, 2)
-            lib_x(2, 1)
-            q_z(3)
-            lib_c(2, 0, "S")
-            lib_x(3, 0)
-            widen(3, 1)
-            q_x(4, 1)
-            lib_c(2, 1, "S")
-            mm("P", 1, 3)
-            lib_c(3, 0, "S")
-            widen(4, 0)
-            mm("P", 0, 0)
-            q_a(4, 1)
-            lib_x(3, 1)
-            mm("P", 0, 1)
-            lib_z(2)
-            mm("P", 0, 2)
-            lib_c(3, 1, "S")
-            widen(4, 1)
-            mm("P", 0, 3)
-            mm("P", 2, 0)
-            e_p(1, "S")
-            mm("P", 2, 1)
-            mm("P", 2, 2)
-            q_z(4)
-            e_p(0, "S")
-            mm("P", 2, 3)
-            q_x(5, 0)
-            widen(5, 0)
-            e_p(2, "S")
-            mm("M", 0, 0)
-            q_a(5, 0)
-            widen(5, 1)
-            mm("M", 1, 0)
-            mm("M", 2, 0)
-            lib_x(5, 0)
-            lib_z(3)
-            q_x(5, 1)
-            lib_c(5, 0, "S")
-            widen(6, 0)
-            lib_x(5, 1)
-            q_a(5, 1)
-            lib_x(4, 0)
-            lib_x(4, 1)
-            lib_c(5, 1, "V")
-            q_x(6, 0)
-            lib_c(4, 0, "S")
-            widen(6, 1)
-            lib_x(6, 0)
-            lib_c(4, 1, "S")
-            q_x(6, 1)
-            lib_z(5)
-            q_a(6, 0)
-            lib_z(4)
-            lib_x(6, 1)
-            q_a(6, 1)
-            q_z(5)
-            q_x(7, 0)
-            widen(9, 0)
-            q_x(7, 1)
-            q_a(7, 0)
-            mm("M", 0, 1)
-            q_z(6)
-            q_a(7, 1)
-            widen(9, 1)
-            mm("M", 1, 1)
-            mm("M", 0, 2)
-            mm("M", 1, 2)
-            widen(10, 0)
-            lib_c(6, 0, "S")
-            mm("M", 2, 1)
-            mm("M", 2, 2)
-            lib_c(6, 1, "S")
-            lib_x(9, 0)
-            q_z(7)
-            lib_x(9, 1)
-            lib_c(9, 0, "S")
-            lib_z(6)
-            lib_x(10, 0)
-            mm("M", 0, 3)
-            lib_c(9, 1, "S")
-            widen(10, 1)
-            mm("M", 1, 3)
-            lib_c(10, 0, "S")
-            mm("M", 2, 3)
-            e_m(0)
-            lib_x(10, 1)
-            e_m(1)
-            fin_w(0, "S")
-            mm("P", 5, 0)
-            e_m(2)
-            mm("P", 5, 1)
-            lib_c(10, 1, "S")
-            mm("P", 5, 2)
-            fin_w(1, "V")
-            mm("P", 5, 3)
-            fin_w(2, "S")
-            widen(8, 0)
-            mm("M", 4, 0)
-            mm("M", 4, 1)
-            e_p(5, "S")
-            mm("M", 4, 2)
-            mm("M", 4, 3)
-            widen(8, 1)
-            mm("M", 3, 0)
-            mm("M", 3, 1)
-            mm("M", 3, 2)
-            widen(7, 0)
-            mm("M", 3, 3)
-            mm("P", 3, 0)
-            mm("P", 3, 1)
-            widen(7, 1)
-            mm("P", 3, 2)
-            mm("P", 3, 3)
-            lib_x(8, 0)
-            e_p(3, "S")
-            lib_z(10)
-            lib_x(8, 1)
-            lib_c(8, 0, "S")
-            lib_x(7, 0)
-            lib_z(9)
-            mm("P", 4, 0)
-            lib_c(8, 1, "S")
-            e_m(3)
-            mm("P", 4, 1)
-            mm("P", 4, 2)
-            lib_c(7, 0, "S")
-            widen(11, 0)
-            mm("P", 4, 3)
-            mm("P", 10, 0)
-            fin_w(3, "S")
-            mm("P", 10, 1)
-            mm("P", 10, 2)
-            e_p(4, "S")
-            lib_z(8)
-            mm("P", 10, 3)
-            lib_x(11, 0)
-            widen(11, 1)
-            e_p(10, "S")
-            mm("P", 8, 0)
-            lib_c(11, 0, "S")
-            mm("P", 8, 1)
-            widen(12, 0)
-            mm("P", 8, 2)
-            mm("P", 8, 3)
-            mm("M", 5, 0)
-            e_p(8, "S")
-            mm("M", 5, 1)
-            widen(12, 1)
-            mm("M", 5, 2)
-            mm("M", 5, 3)
-            lib_x(11, 1)
-            widen(13, 0)
-            lib_x(12, 0)
-            lib_c(11, 1, "S")
-            lib_x(12, 1)
-            e_m(5)
-            mm("M", 6, 0)
-            lib_c(12, 0, "S")
-            mm("M", 6, 1)
-            lib_z(11)
-            lib_c(12, 1, "S")
-            mm("M", 6, 2)
-            mm("M", 6, 3)
-            fin_w(5, "V")
-            mm("P", 6, 0)
-            widen(13, 1)
-            mm("P", 6, 1)
-            mm("P", 6, 2)
-            mm("P", 6, 3)
-            lib_z(12)
-            lib_x(7, 1)
-            e_p(6, "S")
-            lib_x(13, 0)
-            e_m(4)
-            lib_c(7, 1, "S")
-            lib_x(13, 1)
-            e_m(6)
-            mm("M", 12, 0)
-            fin_w(4, "S")
-            mm("M", 12, 1)
-            lib_z(7)
-            mm("M", 12, 2)
-            fin_w(6, "S")
-            mm("M", 12, 3)
-            lib_c(13, 0, "V")
-            mm("P", 12, 0)
-            lib_c(13, 1, "S")
-            mm("P", 7, 0)
-            widen(14, 0)
-            mm("P", 7, 1)
-            mm("P", 7, 2)
-            mm("P", 7, 3)
-            lib_z(13)
-            mm("P", 12, 1)
-            e_p(7, "S")
-            mm("P", 12, 2)
-            widen(14, 1)
-            mm("P", 12, 3)
-            lib_x(14, 0)
-            e_p(12, "S")
-            mm("M", 7, 0)
-            widen(15, 0)
-            lib_c(14, 0, "S")
-            mm("M", 7, 1)
-            mm("M", 7, 2)
-            mm("M", 7, 3)
-            e_m(12)
-            mm("P", 13, 0)
-            mm("P", 13, 1)
-            e_m(7)
-            mm("P", 13, 2)
-            fin_w(12, "S")
-            mm("P", 13, 3)
-            widen(15, 1)
-            mm("P", 11, 0)
-            fin_w(7, "S")
-            mm("P", 11, 1)
-            mm("P", 11, 2)
-            e_p(13, "S")
-            mm("P", 11, 3)
-            lib_x(14, 1)
-            e_p(11, "S")
-            lib_x(15, 0)
-            lib_c(14, 1, "V")
-            lib_x(15, 1)
-            lib_c(15, 0, "S")
-            mm("M", 8, 0)
-            lib_c(15, 1, "V")
-            mm("M", 8, 1)
-            mm("M", 8, 2)
-            lib_z(14)
-            mm("M", 8, 3)
-            mm("P", 9, 0)
-            lib_z(15)
-            mm("P", 9, 1)
-            mm("P", 9, 2)
-            e_m(8)
-            mm("P", 9, 3)
-            mm("P", 15, 0)
-            e_p(9, "S")
-            mm("P", 15, 1)
-            fin_w(8, "V")
-            mm("P", 15, 2)
-            mm("P", 15, 3)
-            mm("M", 10, 0)
-            e_p(15, "S")
-            mm("M", 10, 1)
-            mm("M", 10, 2)
-            mm("M", 10, 3)
-            mm("M", 9, 0)
-            e_m(10)
-            mm("M", 9, 1)
-            mm("M", 9, 2)
-            mm("M", 9, 3)
-            fin_w(10, "S")
-            mm("P", 14, 0)
-            e_m(9)
-            mm("P", 14, 1)
-            mm("P", 14, 2)
-            mm("P", 14, 3)
-            fin_w(9, "S")
-            mm("M", 13, 0)
-            e_p(14, "V")
-            mm("M", 13, 1)
-            mm("M", 13, 2)
-            mm("M", 13, 3)
-            mm("M", 11, 0)
-            e_m(13)
-            mm("M", 11, 1)
-            mm("M", 11, 2)
-            mm("M", 11, 3)
-            fin_w(13, "S")
-            mm("M", 15, 0)
-            e_m(11)
-            mm("M", 15, 1)
-            mm("M", 15, 2)
-            mm("M", 15, 3)
-            fin_w(11, "S")
-            mm("M", 14, 0)
-            e_m(15)
-            mm("M", 14, 1)
-            mm("M", 14, 2)
-            mm("M", 14, 3)
-            fin_w(15, "S")
-            e_m(14)
-            fin_w(14, "S")
+            load_query(0)
+            nc.sync.dma_start(out=scale[:], in_=lib_scale.rearrange("(p i) j -> p i j", i=TILES))
+            nc.sync.dma_start(out=weight_in[:], in_=row_weight.rearrange("(p i) -> p i", i=TILES))
+            load_lib(0)
+            for n in range(1, CHUNKS):
+                load_query(n)
+                load_lib(n)
+            for i in range(CHUNKS, TILES):
+                load_lib(i)
+
+            turn_query(0)
+            root_query(0)
+            widen_up_to(1)
+            nc.vector.tensor_copy(out=weight[:], in_=weight_in[:])
+            for c in range(CHUNKS):
+                if c + 1 < CHUNKS:
+                    turn_query(c + 1)
+                multiply_plain(range(TILES))
+                if c + 1 < CHUNKS:
+                    root_query(c + 1)
+                weigh()
+                quantise_lib()
+                copy_lib()
+                save_plain()
+                turn_lib()
+                take_better()
+                widen_up_to(WIDENED_BY_CHUNK[c])
+                multiply_moved(range(TILES))
+                quantise_query(c)
+            while passes_done["moved"][TILES - 1] < PASSES:
+                next_plain = len([n for n in passes_done["plain"] if n == PASSES])
+                quantise_lib()
+                turn_lib()
+                weigh()
+                save_plain()
+                take_better()
+                widen_up_to(2 * (next_plain + WIDEN_AHEAD + STEP_TILES))
+                next_moved = len([n for n in passes_done["moved"] if n == PASSES])
+                multiply_moved(range(next_moved, min(next_moved + STEP_TILES, next_plain)))
+                multiply_plain(range(next_plain, min(next_plain + STEP_TILES, TILES)))
+                copy_lib()
+            take_better()
+            weigh()
+            finish_last()

from contextlib import ExitStack

import concourse.mybir as mybir
from concourse.masks import make_identity

FLOPS = 2 * 2 * 2048 * 512 * 2048

F32 = mybir.dt.float32
BF16 = mybir.dt.bfloat16
U32 = mybir.dt.uint32
U8 = mybir.dt.uint8
FP8 = mybir.dt.float8_e4m3fn
FP8X4 = mybir.dt.float8_e4m3fn_x4
ACT = mybir.ActivationFunctionType
ALU = mybir.AluOpType

P = 128
K = 2048
QUERIES = 512
K_PASS = 512
PASSES = K // K_PASS
TILES = 2048 // P
HALVES = 2 * TILES
CHUNKS = 2 * PASSES
SCALE_K = 128
SCALES = K // SCALE_K

TURN_BANKS = 5
PRODUCT_BANKS = 3

WIDENED_BY_CHUNK = (2, 3, 4, 4, 4, 6, 9, 9)
VECTOR_HALVES = 6
STEP_TILES = 2
WIDEN_AHEAD = 2
LAST_PARTS = 2


def tile_modified_spectrum_search_d1_kernel(tc, lib_bytes, lib_scale, q, q_mod, row_weight, out):
    nc = tc.nc
    lib_rows = lib_bytes.rearrange("(p i) k -> p i k", i=TILES)
    out_rows = out.rearrange("(p i) b -> p i b", i=TILES)

    with ExitStack() as ctx:
        const = ctx.enter_context(tc.tile_pool(name="const", bufs=1))
        inputs = ctx.enter_context(tc.tile_pool(name="inputs", bufs=TILES))
        work = ctx.enter_context(tc.tile_pool(name="work", bufs=4))
        codes = ctx.enter_context(tc.tile_pool(name="codes", bufs=TILES))
        ends = ctx.enter_context(tc.tile_pool(name="ends", bufs=6))
        turn_psum = ctx.enter_context(tc.psum_pool(name="turn_psum", bufs=TURN_BANKS))
        product_psum = ctx.enter_context(tc.psum_pool(name="product_psum", bufs=PRODUCT_BANKS))

        ident = const.tile([P, P], F32, name="ident")
        make_identity(nc, ident[:])
        scale = const.tile([P, TILES, SCALES], F32, name="scale")
        weight_in = const.tile([P, TILES], BF16, name="weight_in")
        weight = const.tile([P, TILES], F32, name="weight")

        raw_query, query_bank, roots, query_codes = {}, {}, {}, {}
        lib_in, wide, lib_bank, grouped, lib_codes = {}, {}, {}, {}, {}
        plain_bank, plain, moved_bank, better = {}, {}, {}, {}
        done = {"widened": 0, "turned": 0, "copied": 0, "quantised": 0, "query_halves": 0, "root_halves": 0}
        passes_done = {"plain": [0] * TILES, "moved": [0] * TILES}
        weighed = set()

        def load_query(c):
            source = (q if c < PASSES else q_mod).rearrange("(b p) k -> p b k", p=P)
            k0 = K_PASS * (c % PASSES)
            for h in (0, 1):
                raw = inputs.tile([P, 2, K_PASS], BF16, name="raw_query", align_bytes=64)
                nc.sync.dma_start(out=raw[:], in_=source[:, 2 * h : 2 * h + 2, k0 : k0 + K_PASS])
                raw_query[c, h] = raw

        def load_lib(i):
            bytes_in = inputs.tile([P, K], U8, name="bytes_in", align_bytes=64)
            nc.sync.dma_start(out=bytes_in[:], in_=lib_rows[:, i, :])
            lib_in[i] = bytes_in

        def turn_query(c):
            for h in (0, 1):
                bank = turn_psum.tile([P, 2, 2, P], F32, name="turn_bank")
                pairs = raw_query[c, h][:].rearrange("p b k -> p (b k)").bitcast(F32)
                for b in (0, 1):
                    for u in (0, 1):
                        first = 256 * b
                        nc.tensor.transpose(bank[:, u, b, :], pairs[:, first + u : first + 256 : 2], ident[:])
                query_bank[c, h] = bank
                done["query_halves"] += 1

        def root_query(c):
            roots[c] = work.tile([P, 4 * QUERIES], BF16, name="roots", align_bytes=64)
            for h in (0, 1):
                values = query_bank[c, h][:].rearrange("p u b r -> p (u b r)").bitcast(BF16)
                nc.scalar.activation(
                    roots[c][:, 1024 * h : 1024 * h + 1024].rearrange("p (r u e) -> p r u e", u=2, e=2),
                    values.rearrange("p (u r e) -> p r u e", u=2, e=2),
                    ACT.Sqrt,
                )
                done["root_halves"] += 1

        def quantise_query(c):
            words = const.tile([P, QUERIES], U32, name="query_words%d" % c, align_bytes=64)
            planes = const.tile([P, QUERIES], U8, name="query_planes%d" % c, align_bytes=64)
            nc.vector.quantize_mx(out=words[:].bitcast(FP8X4), scales=planes[:], in_=roots[c][:])
            query_codes[c] = (words, planes)

        def widen_up_to(halves):
            while done["widened"] < min(halves, HALVES):
                i, h = divmod(done["widened"], 2)
                if h == 0:
                    wide[i] = work.tile([P, PASSES, 2, P, 2], BF16, name="wide", align_bytes=64)
                for j in range(8 * h, 8 * h + 8):
                    g, part = divmod(j, 4)
                    nc.vector.tensor_scalar(
                        out=wide[i][:, g, :, 32 * part : 32 * part + 32, :].rearrange("p u w e -> p w u e"),
                        in0=lib_in[i][:, SCALE_K * j : SCALE_K * j + SCALE_K]
                        .bitcast(FP8)
                        .rearrange("p (w u e) -> p w u e", u=2, e=2),
                        scalar1=scale[:, i, j : j + 1],
                        scalar2=None,
                        op0=ALU.mult,
                    )
                done["widened"] += 1

        def turn_lib():
            while (
                done["turned"] < done["widened"]
                and done["turned"] + done["query_halves"] - done["copied"] - done["root_halves"] < TURN_BANKS
            ):
                i, h = divmod(done["turned"], 2)
                bank = turn_psum.tile([P, 2, 2, P], F32, name="turn_bank")
                pairs = wide[i][:].rearrange("p g u w e -> p (g u w e)").bitcast(F32)
                for b in (0, 1):
                    for u in (0, 1):
                        first = 256 * (2 * h + b) + P * u
                        nc.tensor.transpose(bank[:, u, b, :], pairs[:, first : first + P], ident[:])
                lib_bank[i, h] = bank
                done["turned"] += 1

        def copy_lib():
            while done["copied"] < done["turned"]:
                i, h = divmod(done["copied"], 2)
                if h == 0:
                    grouped[i] = work.tile([P, 4 * PASSES * P], BF16, name="grouped", align_bytes=64)
                target = grouped[i][:, 1024 * h : 1024 * h + 1024].bitcast(F32).rearrange("p (r u) -> p r u", u=2)
                source = lib_bank[i, h][:].rearrange("p u b r -> p (b r) u")
                if done["copied"] < VECTOR_HALVES:
                    nc.vector.tensor_copy(out=target, in_=source)
                else:
                    nc.scalar.copy(target, source)
                done["copied"] += 1

        def quantise_lib():
            while done["quantised"] < done["copied"] // 2:
                i = done["quantised"]
                words = codes.tile([P, PASSES * P], U32, name="lib_words", align_bytes=64)
                planes = codes.tile([P, PASSES * P], U8, name="lib_planes", align_bytes=64)
                nc.vector.quantize_mx(out=words[:].bitcast(FP8X4), scales=planes[:], in_=grouped[i][:])
                lib_codes[i] = (words, planes)
                done["quantised"] += 1

        def moved_columns(i):
            parts = LAST_PARTS if i == TILES - 1 else 1
            width = QUERIES // parts
            return [slice(width * part, width * (part + 1)) for part in range(parts)]

        def multiply(bank, i, g, c, columns):
            words, planes = lib_codes[i]
            query_words, query_planes = query_codes[c]
            nc.tensor.matmul_mx(
                out=bank,
                lhsT=words[:, P * g : P * g + P].bitcast(FP8X4),
                lhsT_scale=planes[:, P * g : P * g + P],
                rhs=query_words[:, columns].bitcast(FP8X4),
                rhs_scale=query_planes[:, columns],
                start=(g == 0),
                stop=(g == PASSES - 1),
            )

        def multiply_plain(tiles):
            for i in tiles:
                while passes_done["plain"][i] < PASSES and i < done["quantised"] and passes_done["plain"][i] in query_codes:
                    g = passes_done["plain"][i]
                    if g == 0:
                        plain_bank[i] = product_psum.tile([P, QUERIES], F32, name="product_bank")
                    multiply(plain_bank[i][:], i, g, g, slice(0, QUERIES))
                    passes_done["plain"][i] += 1

        def multiply_moved(tiles):
            for i in tiles:
                if i < done["quantised"]:
                    first, last = passes_done["moved"][i], max(0, len(query_codes) - PASSES)
                    for part, columns in enumerate(moved_columns(i)):
                        for g in range(first, last):
                            if g == 0:
                                moved_bank[i, part] = product_psum.tile([P, QUERIES], F32, name="product_bank")
                            width = columns.stop - columns.start
                            multiply(moved_bank[i, part][:, 0:width], i, g, PASSES + g, columns)
                    passes_done["moved"][i] = last

        def save_plain():
            for i in range(TILES):
                if passes_done["plain"][i] == PASSES and i not in plain:
                    plain[i] = ends.tile([P, QUERIES], F32, name="plain")
                    nc.scalar.copy(plain[i][:], plain_bank[i][:])

        def take_better_part(i, part, columns):
            if part == 0:
                better[i] = ends.tile([P, QUERIES], F32, name="better")
            width = columns.stop - columns.start
            nc.vector.tensor_tensor(
                out=better[i][:, columns],
                in0=moved_bank[i, part][:, 0:width],
                in1=plain[i][:, columns],
                op=ALU.max,
            )

        def take_better():
            for i in range(TILES - 1):
                if passes_done["moved"][i] == PASSES and i in plain and i not in better:
                    take_better_part(i, 0, slice(0, QUERIES))

        def weigh():
            for i in range(TILES - 1):
                if i in better and i not in weighed:
                    result = ends.tile([P, QUERIES], F32, name="result")
                    nc.scalar.activation(result[:], better[i][:], ACT.Copy, scale=weight[:, i : i + 1])
                    nc.sync.dma_start(out=out_rows[:, i, :], in_=result[:])
                    weighed.add(i)

        def finish_last():
            i = TILES - 1
            for part, columns in enumerate(moved_columns(i)):
                take_better_part(i, part, columns)
                result = ends.tile([P, QUERIES // LAST_PARTS], F32, name="last_result")
                nc.vector.tensor_scalar(
                    out=result[:], in0=better[i][:, columns], scalar1=weight[:, i : i + 1], scalar2=None, op0=ALU.mult
                )
                nc.sync.dma_start(out=out_rows[:, i, columns], in_=result[:])

        with tc.manual_schedule():
            load_query(0)
            nc.sync.dma_start(out=scale[:], in_=lib_scale.rearrange("(p i) j -> p i j", i=TILES))
            nc.sync.dma_start(out=weight_in[:], in_=row_weight.rearrange("(p i) -> p i", i=TILES))
            load_lib(0)
            for n in range(1, CHUNKS):
                load_query(n)
                load_lib(n)
            for i in range(CHUNKS, TILES):
                load_lib(i)

            turn_query(0)
            root_query(0)
            widen_up_to(1)
            nc.vector.tensor_copy(out=weight[:], in_=weight_in[:])
            for c in range(CHUNKS):
                if c + 1 < CHUNKS:
                    turn_query(c + 1)
                multiply_plain(range(TILES))
                if c + 1 < CHUNKS:
                    root_query(c + 1)
                weigh()
                quantise_lib()
                copy_lib()
                save_plain()
                turn_lib()
                take_better()
                widen_up_to(WIDENED_BY_CHUNK[c])
                multiply_moved(range(TILES))
                quantise_query(c)
            while passes_done["moved"][TILES - 1] < PASSES:
                next_plain = len([n for n in passes_done["plain"] if n == PASSES])
                quantise_lib()
                turn_lib()
                weigh()
                save_plain()
                take_better()
                widen_up_to(2 * (next_plain + WIDEN_AHEAD + STEP_TILES))
                next_moved = len([n for n in passes_done["moved"] if n == PASSES])
                multiply_moved(range(next_moved, min(next_moved + STEP_TILES, next_plain)))
                multiply_plain(range(next_plain, min(next_plain + STEP_TILES, TILES)))
                copy_lib()
            take_better()
            weigh()
            finish_last()
